import numpy as np
import ml_dtypes


def mxq(x, axis, fmt="e4m3"):
    dtype, down = {"e4m3": (ml_dtypes.float8_e4m3fn, 7), "e5m2": (ml_dtypes.float8_e5m2, 14)}[fmt]
    v = np.moveaxis(np.asarray(x, np.float32).astype(ml_dtypes.bfloat16).astype(np.float64), axis, -1)
    blocks = v.reshape(v.shape[:-1] + (-1, 32))
    amax = np.abs(blocks).max(-1, keepdims=True)
    byte = np.maximum(np.where(amax > 0, np.frexp(amax)[1] - 1 + 127, 0) - down, 1)
    scale = np.exp2(byte - 127.0)
    codes = (blocks / scale).astype(np.float32).astype(dtype).astype(np.float64)
    return np.moveaxis((codes * scale).reshape(v.shape), -1, axis)


WIDE = False


def mx_kscale(k):
    if not WIDE:
        return np.ones(k)
    levels = np.array([10, -10, 5, -5, 0])
    if k % 512:
        return np.exp2(np.random.permutation(np.resize(levels, k // 32))).repeat(32)
    a = np.empty((k // 512, 16))
    for p in range(k // 512):
        a[p, :8] = np.random.permutation(np.resize(levels, 8))
        for g in range(8):
            far = levels[np.abs(levels - a[p, g]) >= 10]
            a[p, g + 8] = far[np.random.randint(len(far))]
    return np.exp2(a.ravel()).repeat(32)


BF16 = ml_dtypes.bfloat16


def bf(x):
    return np.asarray(x, np.float32).astype(BF16)


def f64(x):
    return np.asarray(x).astype(np.float64)


T, H, C, E, N = 512, 4, 512, 4, 1024
HC = H * C


def erf(v):
    flat = v.reshape(-1)
    res = np.empty(flat.shape)
    step = 16384
    for i in range(0, flat.size, step):
        c = np.clip(flat[i:i + step], -6.0, 6.0)
        sq = c * c
        q = 2.0 * sq
        tot = np.ones(c.shape)
        for n in range(150, 0, -1):
            tot *= q
            tot /= 2.0 * n + 1.0
            tot += 1.0
        val = 2.0 / np.sqrt(np.pi) * np.exp(-sq) * c * tot
        res[i:i + step] = np.where(np.abs(c) >= 6.0, np.sign(c), val)
    return res.reshape(v.shape)


def exact_gelu(z):
    return 0.5 * z * (1.0 + erf(z / np.sqrt(2.0)))


def softmax(v):
    e = np.exp(v - v.max(-1, keepdims=True))
    return e / e.sum(-1, keepdims=True)


def draw0():
    a, t = mx_kscale(C), mx_kscale(HC)
    return {"x": bf(np.random.standard_normal((T, H, C)) * a),
            "wr": bf(np.random.standard_normal((C, E)) / np.sqrt(C) / a[:, None]),
            "w": bf(np.random.standard_normal((E, C, C)) / np.sqrt(C) / a[:, None]),
            "be": bf(np.random.standard_normal((E, C)) * 0.3),
            "s": bf(np.random.standard_normal((H, C)) * t.reshape(H, C)),
            "wm": bf(np.random.standard_normal((H, C, N)) / np.sqrt(HC) / t.reshape(H, C)[:, :, None])}


def core(x, wr, w, be, s, wm):
    x, wr, w, be, s, wm = f64(x), f64(wr), f64(w), f64(be), f64(s), f64(wm)
    xq = mxq(x.reshape(T * H, C), 1, "e4m3")
    p = xq @ mxq(w, 1, "e4m3")
    p = p.reshape(E, T, H, C).transpose(1, 2, 0, 3) + be
    g = softmax(np.sum(x[..., None, :] * wr.T, axis=-1))
    m = np.sum(g[..., None] * exact_gelu(p), axis=2)
    r = m * s
    return mxq(r.reshape(T, HC), 1, "e4m3") @ mxq(wm.reshape(HC, N), 0, "e4m3")


def e4m3fn_bytes(y):
    return np.clip(np.asarray(y, np.float64), -448.0, 448.0).astype(np.float32).astype(ml_dtypes.float8_e4m3fn).view(np.uint8)


def e4m3fn_values(b):
    return np.asarray(b, np.uint8).view(ml_dtypes.float8_e4m3fn).astype(np.float64)


def setup_inputs():
    d = draw0()
    x0 = np.asarray(d['w']).astype(np.float64)
    s = (np.max(np.abs(x0), axis=(0, 2), keepdims=True) / 448.0).astype(np.float32)
    out = {}
    for k, v in d.items():
        if k == 'w':
            out['w_bytes'] = e4m3fn_bytes(x0 / s.astype(np.float64))
            out['w_scale'] = s
        else:
            out[k] = v
    return out


def reference(x, wr, w_bytes, w_scale, be, s, wm):
    return core(x, wr, e4m3fn_values(w_bytes) * w_scale.astype(np.float64), be, s, wm)

from contextlib import ExitStack

import concourse.mybir as mybir
from concourse.masks import make_identity

T, H, C, E, N = 512, 4, 512, 4, 1024
P = 128
PACK = 4
TB = T // P

FLOPS = 2 * T * H * C * E * C + 2 * T * H * C * N + 2 * T * H * C * E

F32 = mybir.dt.float32
BF16 = mybir.dt.bfloat16
U32 = mybir.dt.uint32
U8 = mybir.dt.uint8
FP8 = mybir.dt.float8_e4m3fn
FP8X4 = mybir.dt.float8_e4m3fn_x4
ACT = mybir.ActivationFunctionType
OP = mybir.AluOpType
AX = mybir.AxisListType

LOG2E = 1.4426950408889634


def tile_multiheadsubtokenmoemerge_kernel(tc, x, wr, w_bytes, w_scale, be, s, wm, out):
    nc = tc.nc
    with ExitStack() as ctx:
        keep = ctx.enter_context(tc.tile_pool(name="keep", bufs=1))
        work = ctx.enter_context(tc.tile_pool(name="work", bufs=2))
        psum = ctx.enter_context(tc.psum_pool(name="psum", bufs=4))
        ctx.enter_context(tc.manual_schedule())

        w_raw = []
        x_sb = []
        wm_raw = []
        for e in range(E):
            w_raw_e = keep.tile([P, PACK, C], U8, name=f"w_raw{e}", align_bytes=64)
            w_raw.append(w_raw_e)
        for b in range(TB):
            x_sb_b = keep.tile([P, H * C], BF16, name=f"x_sb{b}", align_bytes=64)
            x_sb.append(x_sb_b)
        for h in range(H):
            wm_raw_h = keep.tile([P, PACK, N], BF16, name=f"wm_raw{h}", align_bytes=64)
            wm_raw.append(wm_raw_h)
        w_sc = keep.tile([P, PACK], F32, name="w_sc")
        be_bf = keep.tile([P, E, PACK], BF16, name="be_bf")
        be_sb = keep.tile([P, E, PACK], F32, name="be_sb")
        wr_sb = keep.tile([P, PACK, E], BF16, name="wr_sb")
        s_sb = keep.tile([P, H, PACK], BF16, name="s_sb")

        def load_w(e):
            nc.sync.dma_start(out=w_raw[e][:], in_=w_bytes[e].rearrange("(p t) n -> p t n", t=PACK))

        def load_x(b, h0, h1):
            nc.sync.dma_start(
                out=x_sb[b][:, h0 * C : h1 * C],
                in_=x[b * P : (b + 1) * P, h0:h1, :].rearrange("p h c -> p (h c)"),
            )

        def load_wm(h):
            nc.sync.dma_start(out=wm_raw[h][:], in_=wm[h].rearrange("(p t) n -> p t n", t=PACK))

        nc.scalar.dma_start(out=w_sc[:], in_=w_scale.rearrange("o (p t) q -> p (o t q)", t=PACK))
        nc.scalar.dma_start(out=be_bf[:], in_=be.rearrange("e (p t) -> p e t", t=PACK))
        nc.scalar.dma_start(out=wr_sb[:], in_=wr.rearrange("(p t) e -> p t e", t=PACK))
        nc.scalar.dma_start(out=s_sb[:], in_=s.rearrange("h (p t) -> p h t", t=PACK))
        load_w(0)
        load_x(0, 0, 2)
        load_x(0, 2, 4)
        load_x(1, 0, 4)
        load_w(1)
        load_x(2, 0, 4)
        load_x(3, 0, 4)
        load_w(2)
        load_w(3)
        for h in range(H):
            load_wm(h)

        ident = keep.tile([P, P], F32, name="ident")
        make_identity(nc, ident[:])
        two = keep.tile([P, H, E], F32, name="two")
        nc.gpsimd.memset(two[:], 2.0)
        warm = keep.tile([P, 1], F32, name="warm")
        nc.gpsimd.memset(warm[:], 0.0)
        warm_out = keep.tile([P, 1], F32, name="warm_out")
        nc.scalar.activation(out=warm_out[:], in_=warm[:], func=ACT.Gelu)

        w_codes = []
        w_scales = []
        w_wide = {}
        w_int = {}

        def w_widen(e, t, eng):
            if e not in w_wide:
                tile = work.tile([P, PACK, C], BF16, name="w_wide", align_bytes=64, bufs=3)
                w_wide[e] = tile
            src = w_raw[e][:, t, :].bitcast(FP8)
            if eng == "v":
                nc.vector.tensor_scalar(
                    out=w_wide[e][:, t, :], in0=src, scalar1=w_sc[:, t : t + 1], scalar2=None, op0=OP.mult
                )
            else:
                nc.scalar.activation(
                    out=w_wide[e][:, t, :], in_=src, func=ACT.Copy, scale=w_sc[:, t : t + 1]
                )

        def w_interleave(e):
            tile = work.tile([P, C, PACK], BF16, name="w_int", align_bytes=64, bufs=2)
            w_int[e] = tile
            nc.vector.tensor_copy(
                out=tile[:].rearrange("p (t m) j -> p t m j", t=PACK),
                in_=w_wide[e][:].rearrange("p j (m t) -> p t m j", t=PACK),
            )

        def w_quant(e):
            codes = keep.tile([P, C], U32, name=f"w_codes{e}", align_bytes=64)
            scales = keep.tile([P, C], U8, name=f"w_scales{e}", align_bytes=64)
            nc.vector.quantize_mx(
                out=codes[:].bitcast(FP8X4), scales=scales[:], in_=w_int[e][:].rearrange("p c j -> p (c j)")
            )
            w_codes.append(codes)
            w_scales.append(scales)

        x_int = {}
        x_codes = {}
        x_scales = {}
        gate = {}
        logit_tiles = {}
        pow_tiles = {}

        def x_transpose(b, g):
            if g == 0:
                tile = work.tile([P, H * P, PACK], BF16, name="x_int", align_bytes=64, bufs=4)
                x_int[b] = tile
            bank = psum.tile([P, 2, 2, P], F32, name="q", tag="q")
            for i in range(2):
                words = x_sb[b][:, (2 * g + i) * C : (2 * g + i + 1) * C].bitcast(F32)
                for u in range(2):
                    nc.tensor.transpose(bank[:, i, u, :], words[:, u : C // 2 : 2], ident[:])
            dst = x_int[b][:, 2 * g * P : (2 * g + 2) * P, :].rearrange("p r j -> p (r j)").bitcast(F32)
            nc.scalar.copy(
                out=dst.rearrange("p (i r u) -> p i r u", i=2, u=2),
                in_=bank[:].rearrange("p i u r -> p i r u"),
            )

        def x_quant(b):
            codes = work.tile([P, H * P], U32, name="x_codes", align_bytes=64, bufs=4)
            scales = work.tile([P, H * P], U8, name="x_scales", align_bytes=64, bufs=4)
            nc.vector.quantize_mx(
                out=codes[:].bitcast(FP8X4), scales=scales[:], in_=x_int[b][:].rearrange("p r j -> p (r j)")
            )
            x_codes[b] = codes
            x_scales[b] = scales

        def router(b):
            bank = psum.tile([P, H, E], F32, name="q", tag="q")
            for h in range(H):
                for t in range(PACK):
                    nc.tensor.matmul(
                        out=bank[:, h, :],
                        lhsT=x_int[b][:, h * P : (h + 1) * P, t],
                        rhs=wr_sb[:, t, :],
                        start=(t == 0),
                        stop=(t == PACK - 1),
                    )
            logit_tiles[b] = bank

        def softmax_a(b):
            top = work.tile([P, H], F32, name="top")
            nc.vector.reduce_max(out=top[:], in_=logit_tiles[b][:], axis=AX.X)
            diff = work.tile([P, H, E], F32, name="diff")
            nc.vector.tensor_tensor(
                out=diff[:],
                in0=logit_tiles[b][:],
                in1=top[:].unsqueeze(2).to_broadcast([P, H, E]),
                op=OP.subtract,
            )
            expo = work.tile([P, H, E], F32, name="expo")
            nc.gpsimd.tensor_scalar(
                out=expo[:], in0=diff[:], scalar1=LOG2E, scalar2=0.0, op0=OP.mult, op1=OP.add
            )
            power = work.tile([P, H, E], F32, name="power", bufs=4)
            nc.gpsimd.tensor_tensor(out=power[:], in0=two[:], in1=expo[:], op=OP.pow)
            pow_tiles[b] = power

        def softmax_b(b):
            total = work.tile([P, H], F32, name="total")
            nc.vector.reduce_sum(out=total[:], in_=pow_tiles[b][:], axis=AX.X)
            inv = work.tile([P, H], F32, name="inv")
            nc.vector.reciprocal(out=inv[:], in_=total[:])
            g = work.tile([P, H, E], F32, name="gate", bufs=4)
            nc.vector.tensor_tensor(
                out=g[:], in0=pow_tiles[b][:], in1=inv[:].unsqueeze(2).to_broadcast([P, H, E]), op=OP.mult
            )
            gate[b] = g

        wm_codes = {}
        wm_scales = {}
        wm_int = {}

        def wm_interleave(h):
            tile = work.tile([P, N, PACK], BF16, name="wm_int", align_bytes=64, bufs=3)
            wm_int[h] = tile
            step = 256
            for n0 in range(0, N, step):
                nc.gpsimd.tensor_scalar(
                    out=tile[:, n0 : n0 + step, :],
                    in0=wm_raw[h][:, :, n0 : n0 + step].rearrange("p j n -> p n j"),
                    scalar1=1.0,
                    scalar2=0.0,
                    op0=OP.mult,
                    op1=OP.add,
                )

        def wm_quant(h, half):
            if half == 0:
                codes = keep.tile([P, N], U32, name=f"wm_codes{h}", align_bytes=64)
                scales = keep.tile([P, N], U8, name=f"wm_scales{h}", align_bytes=64)
                wm_codes[h] = codes
                wm_scales[h] = scales
            cols = slice(half * 512, half * 512 + 512)
            nc.vector.quantize_mx(
                out=wm_codes[h][:, cols].bitcast(FP8X4),
                scales=wm_scales[h][:, cols],
                in_=wm_int[h][:, cols, :].rearrange("p n j -> p (n j)"),
            )

        gelus = {}
        acc = {}

        banks = {}

        def mx1(k):
            b, e = k
            for t in range(PACK):
                bank = psum.tile([P, H * P], F32, name="p", tag="p")
                nc.tensor.matmul_mx(
                    out=bank[:],
                    lhsT=w_codes[e][:, t * P : (t + 1) * P].bitcast(FP8X4),
                    lhsT_scale=w_scales[e][:, t * P : (t + 1) * P],
                    rhs=x_codes[b][:].bitcast(FP8X4),
                    rhs_scale=x_scales[b][:],
                    start=True,
                    stop=True,
                )
                banks[(k, t)] = bank

        def gelu(k, t):
            e = k[1]
            ge = work.tile([P, H * P], F32, name="ge", bufs=10)
            nc.scalar.activation(out=ge[:], in_=banks[(k, t)][:], func=ACT.Gelu, bias=be_sb[:, e, t : t + 1])
            gelus[(k, t)] = ge

        def turn(k, h):
            bank = psum.tile([P, PACK * P], F32, name="q", tag="q")
            for t in range(PACK):
                nc.tensor.transpose(
                    bank[:, t * P : (t + 1) * P], gelus[(k, t)][:, h * P : (h + 1) * P], ident[:]
                )
            return bank

        def gating(k, h, bank):
            b, e = k
            new = work.tile([P, PACK * P], F32, name="acc", bufs=13)
            g = gate[b][:, h, e : e + 1]
            if e == 0:
                nc.scalar.activation(out=new[:], in_=bank[:], func=ACT.Copy, scale=g)
            else:
                nc.vector.scalar_tensor_tensor(
                    out=new[:], in0=bank[:], scalar=g, in1=acc[(b, h)][:], op0=OP.mult, op1=OP.add
                )
            acc[(b, h)] = new

        r_tiles = {}
        r_codes = {}
        r_scales = {}

        def back(b, h):
            bank = psum.tile([P, PACK, P], F32, name="q", tag="q")
            for t in range(PACK):
                nc.tensor.transpose(bank[:, t, :], acc[(b, h)][:, t * P : (t + 1) * P], ident[:])
            return bank

        def scale_r(b, h, bank):
            r = work.tile([P, P, PACK], BF16, name="r", align_bytes=64, bufs=4)
            nc.vector.tensor_tensor(
                out=r[:],
                in0=bank[:].rearrange("p t r -> p r t"),
                in1=s_sb[:, h, :].unsqueeze(1).to_broadcast([P, P, PACK]),
                op=OP.mult,
            )
            r_tiles[(b, h)] = r

        def r_quant(b, h):
            codes = work.tile([P, P], U32, name="r_codes", align_bytes=64, bufs=12)
            scales = work.tile([P, P], U8, name="r_scales", align_bytes=64, bufs=12)
            nc.vector.quantize_mx(
                out=codes[:].bitcast(FP8X4), scales=scales[:], in_=r_tiles[(b, h)][:].rearrange("p r j -> p (r j)")
            )
            r_codes[(b, h)] = codes
            r_scales[(b, h)] = scales

        def merge_pass(b, h, n, bank):
            cols = slice(n * 512, (n + 1) * 512)
            nc.tensor.matmul_mx(
                out=bank[:],
                lhsT=r_codes[(b, h)][:].bitcast(FP8X4),
                lhsT_scale=r_scales[(b, h)][:],
                rhs=wm_codes[h][:, cols].bitcast(FP8X4),
                rhs_scale=wm_scales[h][:, cols],
                start=(h == 0),
                stop=(h == H - 1),
            )

        def store(b, n, bank):
            res = work.tile([P, 512], F32, name="res", bufs=4)
            if n == 0:
                nc.scalar.copy(out=res[:], in_=bank[:])
            else:
                nc.vector.tensor_copy(out=res[:], in_=bank[:])
            nc.sync.dma_start(out=out[b * P : (b + 1) * P, n * 512 : (n + 1) * 512], in_=res[:])

        def merge(b, n):
            bank = psum.tile([P, 512], F32, name="q", tag="q")
            for h in range(H):
                merge_pass(b, h, n, bank)
            return bank

        w_widen(0, 0, "v")
        w_widen(0, 1, "v")
        w_widen(0, 2, "s")
        w_widen(0, 3, "s")
        w_interleave(0)
        x_transpose(0, 0)
        x_transpose(0, 1)
        w_quant(0)
        nc.vector.tensor_copy(out=be_sb[:], in_=be_bf[:])
        x_quant(0)
        router(0)
        softmax_a(0)
        x_transpose(1, 0)
        x_transpose(1, 1)
        mx1((0, 0))
        router(1)
        gelu((0, 0), 0)
        gelu((0, 0), 1)
        x_quant(1)
        w_widen(1, 0, "v")
        w_widen(1, 1, "v")
        w_widen(1, 2, "v")
        w_widen(1, 3, "v")
        softmax_b(0)
        softmax_a(1)
        w_interleave(1)
        w_quant(1)
        x_transpose(2, 0)
        x_transpose(2, 1)
        router(2)
        gelu((0, 0), 2)
        gelu((0, 0), 3)

        order = [(b, e) for e in range(E) for b in range(2)] + [(b, e) for b in range(2, TB) for e in range(E)]
        order = [(0, 0), (1, 0), (0, 1), (1, 1), (0, 2), (0, 3), (1, 2), (1, 3)] + order[8:]
        merge_at = {9: (0, 0), 10: (0, 1), 12: (1, 0), 13: (1, 1)}
        back_at = {7: [(0, 0), (0, 1)], 8: [(0, 2), (0, 3)], 10: [(1, 0), (1, 1)], 11: [(1, 2), (1, 3)], 14: [(2, 0), (2, 1)], 15: [(2, 2), (2, 3)]}
        for i in range(1, 16):
            k = order[i]
            merged = None
            if i in merge_at:
                merged = merge(merge_at[i][0], merge_at[i][1])
            mx1(k)
            gelu(k, 0)
            gelu(k, 1)
            for h in range(H):
                bank = turn(order[i - 1], h)
                gating(order[i - 1], h, bank)
                if h < 2:
                    gelu(k, 2 + h)
            if i == 1:
                softmax_b(1)
                softmax_a(2)
                x_transpose(3, 0)
                x_transpose(3, 1)
                x_quant(2)
            if i == 2:
                router(3)
                softmax_b(2)
                softmax_a(3)
                x_quant(3)
            if i == 3:
                softmax_b(3)
            if i in (1, 3):
                e = 2 + i // 2
                w_widen(e, 0, "s")
                w_widen(e, 1, "v")
                w_widen(e, 2, "v")
                w_widen(e, 3, "v")
                w_interleave(e)
                w_quant(e)
            if merged is not None:
                store(merge_at[i][0], merge_at[i][1], merged)
            done = back_at.get(i, [])
            for j in range(len(done) + 1):
                if j < len(done):
                    scale_r(done[j][0], done[j][1], back(done[j][0], done[j][1]))
                if j > 0:
                    r_quant(done[j - 1][0], done[j - 1][1])
            if i in (2, 3, 4, 5):
                wm_interleave(i - 2)
            if 5 <= i < 9:
                wm_quant(i - 5, 0)
                wm_quant(i - 5, 1)
        last = TB - 1
        for n in range(2):
            merged = merge(2, n)
            store(2, n, merged)
        o0 = psum.tile([P, 512], F32, name="p", tag="p")
        o1 = psum.tile([P, 512], F32, name="p", tag="p")
        outs = [o0, o1]
        end = (last, E - 1)

        def finish(h):
            r_quant(last, h)
            for n in range(2):
                merge_pass(last, h, n, outs[n])

        gating(end, 0, turn(end, 0))
        gating(end, 1, turn(end, 1))
        scale_r(last, 0, back(last, 0))
        gating(end, 2, turn(end, 2))
        scale_r(last, 1, back(last, 1))
        gating(end, 3, turn(end, 3))
        finish(0)
        scale_r(last, 2, back(last, 2))
        finish(1)
        scale_r(last, 3, back(last, 3))
        finish(2)
        finish(3)
        for n in range(2):
            store(last, n, outs[n])
